import numpy as np
import ml_dtypes


def mxq(x, axis, fmt="e4m3"):
    dtype, down = {"e4m3": (ml_dtypes.float8_e4m3fn, 7), "e5m2": (ml_dtypes.float8_e5m2, 14)}[fmt]
    v = np.moveaxis(np.asarray(x, np.float32).astype(ml_dtypes.bfloat16).astype(np.float64), axis, -1)
    blocks = v.reshape(v.shape[:-1] + (-1, 32))
    amax = np.abs(blocks).max(-1, keepdims=True)
    byte = np.maximum(np.where(amax > 0, np.frexp(amax)[1] - 1 + 127, 0) - down, 1)
    scale = np.exp2(byte - 127.0)
    codes = (blocks / scale).astype(np.float32).astype(dtype).astype(np.float64)
    return np.moveaxis((codes * scale).reshape(v.shape), -1, axis)


WIDE = False


def mx_kscale(k):
    if not WIDE:
        return np.ones(k)
    levels = np.array([10, -10, 5, -5, 0])
    if k % 512:
        return np.exp2(np.random.permutation(np.resize(levels, k // 32))).repeat(32)
    a = np.empty((k // 512, 16))
    for p in range(k // 512):
        a[p, :8] = np.random.permutation(np.resize(levels, 8))
        for g in range(8):
            far = levels[np.abs(levels - a[p, g]) >= 10]
            a[p, g + 8] = far[np.random.randint(len(far))]
    return np.exp2(a.ravel()).repeat(32)


def f64(x):
    return np.asarray(x).astype(np.float64)


def striped(idx):
    return np.tile(idx.reshape(-1, 16).T, (8, 1)).astype(np.uint16)


def unstriped(offs):
    return offs[:16].T.reshape(-1).astype(np.int64)


E2M1 = np.array([0.0, 0.5, 1.0, 1.5, 2.0, 3.0, 4.0, 6.0, -0.0, -0.5, -1.0, -1.5, -2.0, -3.0, -4.0, -6.0])


def pack_weight(w, fmt):
    k, n = w.shape
    w = f64(np.asarray(w, np.float32).astype(ml_dtypes.bfloat16)).reshape(k // 32, 32, n)
    amax = np.abs(w).max(1)
    if fmt == "e4m3":
        byte = np.frexp(amax)[1] - 1 + 127 - 7
    else:
        mant, ex = np.frexp(amax / 6.0)
        byte = np.where(mant > 0.5, ex, ex - 1) + 127
    byte = np.clip(np.where(amax > 0, byte, 1), 1, 254)
    scaled = (w * np.exp2(127.0 - byte)[:, None, :]).reshape(k, n).astype(np.float32)
    by_word = np.ascontiguousarray(scaled.reshape(k // 512, 128, 4, n).transpose(0, 1, 3, 2))
    if fmt == "e4m3":
        words = by_word.astype(ml_dtypes.float8_e4m3fn).view(np.uint8)
    else:
        c = by_word.astype(ml_dtypes.float4_e2m1fn).view(np.uint8) & 0xF
        words = (c[..., 0::2] | (c[..., 1::2] << 4)).reshape(k // 512, 128, 2 * n)
    return np.ascontiguousarray(words), np.ascontiguousarray(byte.astype(np.uint8).reshape(k // 512, 16, n))


def unpack_weight(words, scales, fmt):
    g, _, n = scales.shape
    words = np.ascontiguousarray(words).reshape(g, 128, n, -1)
    if fmt == "e4m3":
        vals = words.view(ml_dtypes.float8_e4m3fn).astype(np.float64)
    else:
        nib = np.empty((g, 128, n, 4), np.uint8)
        nib[..., 0::2] = words & 0xF
        nib[..., 1::2] = words >> 4
        vals = E2M1[nib]
    vals = vals * np.repeat(np.exp2(scales.astype(np.float64) - 127.0), 8, axis=1)[..., None]
    return vals.transpose(0, 1, 3, 2).reshape(g * 512, n)


def planes(y):
    n, m = y.shape
    v = y.astype(np.float32).astype(ml_dtypes.bfloat16).astype(np.float64).reshape(n // 32, 32, m)
    top = np.abs(v).max(1)
    byte = np.clip(np.where(top > 0, np.frexp(top)[1] - 1 + 127 - 7, 1), 1, 254)
    codes = (v * np.exp2(127.0 - byte)[:, None, :]).reshape(n, m).astype(np.float32).astype(ml_dtypes.float8_e4m3fn).view(np.uint8)
    words = codes.reshape(n // 512, 128, 4, m).transpose(0, 1, 3, 2)
    return np.ascontiguousarray(words), np.ascontiguousarray(byte.astype(np.uint8).reshape(n // 512, 16, m))


def d_silu(v):
    s = 1.0 / (1.0 + np.exp(-np.maximum(v, -700.0)))
    return s * (1.0 + v * (1.0 - s))


K, T, E, C, H, N = 512, 768, 3, 256, 512, 1024


def by_expert(wq, xq):
    return np.concatenate([wq[e].T @ xq[:, e * C:(e + 1) * C] for e in range(E)], axis=1)


def setup_inputs():
    n = np.random.standard_normal
    v = mx_kscale(N)
    u = mx_kscale(H)
    slot_token = np.random.permutation(T)[:E * C]
    w_slot = np.random.uniform(0.2, 1.0, E * C)
    dy = pack_weight(n((N, T)) * v[:, None], "e4m3")
    w2t = pack_weight(n((N, H)) / np.sqrt(N) / v[:, None] * u, "e4m3")
    w1t = [pack_weight(m, "e2m1") for m in n((E, H, K)) / np.sqrt(H) / u[None, :, None]]
    return {
        "dy_words": dy[0],
        "dy_scales": dy[1],
        "w2t_words": w2t[0],
        "w2t_scales": w2t[1],
        "w1t_words": np.stack([m[0] for m in w1t]),
        "w1t_scales": np.stack([m[1] for m in w1t]),
        "a": (n((H, E * C))).astype(np.float32),
        "gate": (np.tile(w_slot, (128, 1))).astype(np.float32),
        "offs": striped(slot_token),
    }


def reference(dy_words, dy_scales, w2t_words, w2t_scales, w1t_words, w1t_scales, a, gate, offs):
    w2t = unpack_weight(w2t_words, w2t_scales, "e4m3")
    w1t = np.stack([unpack_weight(w1t_words[e], w1t_scales[e], "e2m1") for e in range(E)])
    idx = unstriped(offs)
    dc = w2t.T @ unpack_weight(dy_words, dy_scales, "e4m3")
    da = f64(gate[:1]) * dc[:, idx] * d_silu(f64(a))
    dx = by_expert(w1t, mxq(da, 0, "e4m3"))
    out = np.zeros((K, T))
    out[:, idx] = dx
    out_0 = out
    return (out_0,) + planes(out_0)

@@ -1,0 +1,234 @@
+from contextlib import ExitStack
+
+import concourse.mybir as mybir
+
+K, T, E, C, H, N = 512, 768, 3, 256, 512, 1024
+FLOPS = 2 * N * H * T + 2 * H * K * E * C
+
+F32 = mybir.dt.float32
+BF16 = mybir.dt.bfloat16
+I32 = mybir.dt.int32
+U16 = mybir.dt.uint16
+U8 = mybir.dt.uint8
+FP8X4 = mybir.dt.float8_e4m3fn_x4
+FP4X4 = mybir.dt.float4_e2m1fn_x4
+ALU = mybir.AluOpType
+ACT = mybir.ActivationFunctionType
+
+P = 128
+PACK = 4
+PASSES = N // (P * PACK)
+BANK = 512
+TOKEN_CUTS = ((0, 512), (512, 768))
+OFFS_COLS = C // 16
+
+
+def tile_moe_sdb_silu_kernel(
+    tc, dy_words, dy_scales, w2t_words, w2t_scales, w1t_words, w1t_scales, a, gate, offs, out_0, out_1, out_2
+):
+    nc = tc.nc
+    with ExitStack() as ctx:
+        sb = ctx.enter_context(tc.tile_pool(name="sb", bufs=1))
+        ps = ctx.enter_context(tc.psum_pool(name="ps", bufs=8))
+
+        def tile(shape, dtype, name):
+            return sb.tile(shape, dtype, name=name, align_bytes=64)
+
+        offsets = sb.tile([P, T // 16], U16, name="offsets")
+        w2_raw = [tile([P, H], I32, f"w2_raw{s}") for s in range(PASSES)]
+        w2_codes = [tile([P, H], I32, f"w2_codes{s}") for s in range(PASSES)]
+        w2s_rows = tile([P, H], U8, "w2s_rows")
+        w2s_raw = tile([P, H], U8, "w2s_raw")
+        w2_scale = tile([P, H], U8, "w2_scale")
+        dy_codes = [tile([P, T], I32, f"dy_codes{s}") for s in range(PASSES)]
+        dy_scale = tile([P, T], U8, "dy_scale")
+        w1_raw = tile([P, E, 2 * K], U8, "w1_raw")
+        w1_codes = tile([P, PACK, 2 * E * P], U8, "w1_codes")
+        w1s_raw = tile([P, E, K], U8, "w1s_raw")
+        w1_scale = tile([P, PACK, E * P], U8, "w1_scale")
+        pre = [tile([P, PACK, C], F32, f"pre{e}") for e in range(E)]
+        sig = [tile([P, PACK * C], F32, f"sig{e}") for e in range(E)]
+        neg_silu = [tile([P, PACK * C], F32, f"neg_silu{e}")[:] for e in range(E)]
+        g = [tile([P, C], F32, f"g{e}") for e in range(E)]
+        minus_g = [tile([P, C], F32, f"minus_g{e}") for e in range(E)]
+        dc = [tile([P, T], F32, f"dc{t}") for t in range(PACK)]
+        y = [tile([P, T], F32, f"y{t}") for t in range(PACK)]
+
+        nc.vector.memset(w2s_raw[:].bitcast(I32), 0)
+        nc.gpsimd.memset(dy_scale[:].bitcast(I32), 0)
+        nc.gpsimd.memset(w1s_raw[:].rearrange("p e k -> p (e k)").bitcast(I32), 0)
+
+        for q in range(4):
+            nc.sync.dma_start(
+                out=w2s_rows[32 * q : 32 * q + 4 * PASSES, :].bitcast(I32),
+                in_=w2t_scales[:, 4 * q : 4 * q + 4, :].bitcast(I32),
+            )
+
+        def load_pass(s):
+            nc.sync.dma_start(out=w2_raw[s][:], in_=w2t_words[s].rearrange("p n d -> p (n d)").bitcast(I32))
+            nc.sync.dma_start(out=dy_codes[s][:], in_=dy_words[s].rearrange("p n d -> p (n d)").bitcast(I32))
+
+        load_pass(0)
+        for q in range(4):
+            nc.sync.dma_start(
+                out=dy_scale[32 * q : 32 * q + 4 * PASSES, :].bitcast(I32),
+                in_=dy_scales[:, 4 * q : 4 * q + 4, :].bitcast(I32),
+            )
+        load_pass(1)
+        nc.sync.dma_start(offsets[:], offs)
+        a_rows = a.rearrange("(p j) c -> p j c", j=PACK)
+        for e in range(E):
+            nc.sync.dma_start(out=g[e][:], in_=gate[:, e * C : (e + 1) * C])
+            nc.sync.dma_start(out=pre[e][:], in_=a_rows[:, :, e * C : (e + 1) * C])
+        nc.sync.dma_start(
+            out=w1_raw[:].bitcast(I32), in_=w1t_words.rearrange("e s p b -> p (e s) b").bitcast(I32)
+        )
+        for q in range(4):
+            nc.sync.dma_start(
+                out=w1s_raw[32 * q : 32 * q + 4, :, :].bitcast(I32),
+                in_=w1t_scales[:, 0, 4 * q : 4 * q + 4, :].rearrange("e r k -> r e k").bitcast(I32),
+            )
+
+        for q in range(4):
+            rows = slice(32 * q, 32 * q + 4 * PASSES)
+            nc.vector.tensor_copy(out=w2s_raw[rows, :].bitcast(I32), in_=w2s_rows[rows, :].bitcast(I32))
+        nc.vector.tensor_copy(
+            out=w2_scale[:].rearrange("p (t m) -> p m t", t=PACK),
+            in_=w2s_raw[:].rearrange("p (m t) -> p m t", t=PACK),
+        )
+        for s in range(PASSES):
+            nc.vector.tensor_copy(
+                out=w2_codes[s][:].rearrange("p (t m) -> p m t", t=PACK),
+                in_=w2_raw[s][:].rearrange("p (m t) -> p m t", t=PACK),
+            )
+        for e in range(E):
+            nc.scalar.activation(sig[e][:], pre[e][:].rearrange("p j c -> p (j c)"), ACT.Sigmoid)
+        for e in range(E):
+            nc.scalar.activation(neg_silu[e], pre[e][:].rearrange("p j c -> p (j c)"), ACT.Silu, scale=-1.0)
+
+        gated = [tile([P, PACK, C], F32, f"gated{e}") for e in range(E - 1)]
+        for e in range(E):
+            nc.gpsimd.tensor_scalar(minus_g[e][:], g[e][:], -1.0, 0.0, ALU.mult, ALU.add)
+            for t in range(PACK if e < E - 1 else 0):
+                nc.gpsimd.tensor_tensor(gated[e][:, t, :], sig[e][:, t * C : (t + 1) * C], minus_g[e][:], ALU.mult)
+
+        first_picked = tile([P, PACK, C], F32, "first_picked")
+        picked = [first_picked, pre[2], first_picked]
+
+        def gather(e, t):
+            window = dc[t][:].indirect(offsets[:, e * OFFS_COLS : (e + 1) * OFFS_COLS])
+            if e == 1:
+                nc.scalar.activation(picked[e][:, t, :], window, ACT.Copy)
+            elif e == 0:
+                nc.vector.tensor_copy(picked[e][:, t, :], window)
+            else:
+                nc.vector.tensor_tensor(picked[e][:, t, :], window, minus_g[e][:], ALU.mult)
+
+        banks = [[ps.tile([P, BANK], F32, name="bank") for cut in TOKEN_CUTS] for t in range(PACK)]
+        for s in range(PASSES):
+            for t in range(PACK):
+                for bank, (lo, hi) in zip(banks[t], TOKEN_CUTS):
+                    nc.tensor.matmul_mx(
+                        out=bank[:, : hi - lo],
+                        lhsT=w2_codes[s][:, t * P : (t + 1) * P].bitcast(FP8X4),
+                        lhsT_scale=w2_scale[4 * s :, t * P : (t + 1) * P],
+                        rhs=dy_codes[s][:, lo:hi].bitcast(FP8X4),
+                        rhs_scale=dy_scale[4 * s :, lo:hi],
+                        start=(s == 0),
+                        stop=(s == PASSES - 1),
+                    )
+        for t in range(PACK):
+            for bank, (lo, hi) in zip(banks[t], TOKEN_CUTS):
+                nc.vector.tensor_copy(out=dc[t][:, lo:hi], in_=bank[:, : hi - lo])
+            gather(0, t)
+
+        nc.vector.tensor_copy(
+            out=w1_codes[:].bitcast(U16).rearrange("p t m -> p m t"),
+            in_=w1_raw[:].bitcast(U16).rearrange("p e (m t) -> p (e m) t", t=PACK),
+        )
+        nc.vector.tensor_copy(
+            out=w1_scale[:].rearrange("p t m -> p m t"),
+            in_=w1s_raw[:].rearrange("p e (m t) -> p (e m) t", t=PACK),
+        )
+
+        dx = [[tile([P, 2, C], F32, f"dx{e}_{h}") for h in range(2)] for e in range(E)]
+
+        def expert(e):
+            minus_d = tile([P, PACK, C], F32, f"minus_d{e}")
+            factor = gated[e][:].rearrange("p j c -> p (j c)") if e < E - 1 else sig[e][:]
+            nc.vector.scalar_tensor_tensor(
+                minus_d[:].rearrange("p j c -> p (j c)"), neg_silu[e], 1.0, factor, ALU.subtract, ALU.mult
+            )
+            if e > 0:
+                for t in range(PACK):
+                    gather(e, t)
+            da = tile([P, C, PACK], BF16, f"da{e}")
+            nc.vector.tensor_tensor(
+                da[:].rearrange("p (c i) t -> p c t i", i=4),
+                picked[e][:].rearrange("p t (c i) -> p c t i", i=4),
+                minus_d[:].rearrange("p t (c i) -> p c t i", i=4),
+                ALU.mult,
+            )
+            da_codes = tile([P, C], I32, f"da_codes{e}")
+            da_scale = tile([P, C], U8, f"da_scale{e}")
+            nc.vector.quantize_mx(
+                out=da_codes[:].bitcast(FP8X4), scales=da_scale[:], in_=da[:].rearrange("p c t -> p (c t)")
+            )
+            for h in range(2):
+                bank = ps.tile([P, BANK], F32, name="bank")
+                for u in range(2):
+                    t = h + 2 * u
+                    nc.tensor.matmul_mx(
+                        out=bank[:, u * C : (u + 1) * C],
+                        lhsT=w1_codes[:, t, 2 * e * P : 2 * (e + 1) * P].bitcast(FP4X4),
+                        lhsT_scale=w1_scale[:, t, e * P : (e + 1) * P],
+                        rhs=da_codes[:].bitcast(FP8X4),
+                        rhs_scale=da_scale[:],
+                        start=True,
+                        stop=True,
+                    )
+                if e > 0 and h == 0:
+                    nc.vector.tensor_copy(out=dx[e][h][:].rearrange("p u c -> p (u c)"), in_=bank[:])
+                else:
+                    nc.scalar.copy(out=dx[e][h][:].rearrange("p u c -> p (u c)"), in_=bank[:])
+
+        def scatter(e, t, on_vector):
+            window = y[t][:].indirect(offsets[:, e * OFFS_COLS : (e + 1) * OFFS_COLS])
+            if on_vector:
+                nc.vector.tensor_copy(window, dx[e][t % 2][:, t // 2, :])
+            else:
+                nc.scalar.activation(window, dx[e][t % 2][:, t // 2, :], ACT.Copy)
+
+        expert(0)
+        for t in range(PACK):
+            scatter(0, t, False)
+        expert(1)
+        expert(2)
+        for e in (1, 2):
+            for t in range(PACK):
+                scatter(e, t, t % 2 == 0)
+
+        out_rows = out_0.rearrange("(p j) c -> p j c", j=PACK)
+        pairs = tile([P, 2, T, 2], BF16, "pairs")
+        for t in range(PACK):
+            nc.sync.dma_start(out=out_rows[:, t, :], in_=y[t][:])
+            nc.vector.tensor_copy(out=pairs[:, t // 2, :, t % 2], in_=y[t][:])
+        y_codes = tile([P, T], I32, "y_codes")
+        y_scale = tile([P, T], U8, "y_scale")
+        out_words = out_1[0].rearrange("p c d -> p (c d)").bitcast(I32)
+        for lo, hi in TOKEN_CUTS:
+            woven = tile([P, hi - lo, 2], I32, f"woven{lo}")
+            nc.vector.tensor_copy(
+                out=woven[:],
+                in_=pairs[:].rearrange("p h c u -> p h (c u)").bitcast(I32)[:, :, lo:hi].rearrange("p h c -> p c h"),
+            )
+            nc.vector.quantize_mx(
+                out=y_codes[:, lo:hi].bitcast(FP8X4),
+                scales=y_scale[:, lo:hi],
+                in_=woven[:].rearrange("p c h -> p (c h)").bitcast(BF16),
+            )
+            nc.sync.dma_start(out=out_words[:, lo:hi], in_=y_codes[:, lo:hi])
+        for q in range(4):
+            nc.scalar.dma_start(
+                out=out_2[0, 4 * q : 4 * q + 4, :].bitcast(I32), in_=y_scale[32 * q : 32 * q + 4, :].bitcast(I32)
+            )

@@ -8,6 +8,7 @@ FLOPS = 2 * N * H * T + 2 * H * K * E * C
 F32 = mybir.dt.float32
 BF16 = mybir.dt.bfloat16
 I32 = mybir.dt.int32
+U32 = mybir.dt.uint32
 U16 = mybir.dt.uint16
 U8 = mybir.dt.uint8
 FP8X4 = mybir.dt.float8_e4m3fn_x4
@@ -31,8 +32,8 @@ def tile_moe_sdb_silu_kernel(
         sb = ctx.enter_context(tc.tile_pool(name="sb", bufs=1))
         ps = ctx.enter_context(tc.psum_pool(name="ps", bufs=8))
 
-        def tile(shape, dtype, name):
-            return sb.tile(shape, dtype, name=name, align_bytes=64)
+        def tile(shape, dtype, name, tag=None):
+            return sb.tile(shape, dtype, name=name, tag=tag or name, align_bytes=64)
 
         offsets = sb.tile([P, T // 16], U16, name="offsets")
         w2_raw = [tile([P, H], I32, f"w2_raw{s}") for s in range(PASSES)]
@@ -45,12 +46,12 @@ def tile_moe_sdb_silu_kernel(
         w1_raw = tile([P, E, 2 * K], U8, "w1_raw")
         w1_codes = tile([P, PACK, 2 * E * P], U8, "w1_codes")
         w1s_raw = tile([P, E, K], U8, "w1s_raw")
-        w1_scale = tile([P, PACK, E * P], U8, "w1_scale")
         pre = [tile([P, PACK, C], F32, f"pre{e}") for e in range(E)]
         sig = [tile([P, PACK * C], F32, f"sig{e}") for e in range(E)]
         neg_silu = [tile([P, PACK * C], F32, f"neg_silu{e}")[:] for e in range(E)]
-        g = [tile([P, C], F32, f"g{e}") for e in range(E)]
-        minus_g = [tile([P, C], F32, f"minus_g{e}") for e in range(E)]
+        g_first = tile([P, C], F32, "g_first")
+        g_rest = tile([P, T - C], F32, "g_rest")
+        minus_g_first = tile([P, C], F32, "minus_g_first")
         dc = [tile([P, T], F32, f"dc{t}") for t in range(PACK)]
         y = [tile([P, T], F32, f"y{t}") for t in range(PACK)]
 
@@ -77,9 +78,11 @@ def tile_moe_sdb_silu_kernel(
         load_pass(1)
         nc.sync.dma_start(offsets[:], offs)
         a_rows = a.rearrange("(p j) c -> p j c", j=PACK)
-        for e in range(E):
-            nc.sync.dma_start(out=g[e][:], in_=gate[:, e * C : (e + 1) * C])
-            nc.sync.dma_start(out=pre[e][:], in_=a_rows[:, :, e * C : (e + 1) * C])
+        nc.sync.dma_start(out=pre[0][:], in_=a_rows[:, :, 0:C])
+        nc.sync.dma_start(out=g_first[:], in_=gate[:, 0:C])
+        nc.sync.dma_start(out=pre[1][:], in_=a_rows[:, :, C : 2 * C])
+        for j in (0, 2):
+            nc.sync.dma_start(out=pre[2][:, j : j + 2, :], in_=a_rows[:, j : j + 2, 2 * C : 3 * C])
         nc.sync.dma_start(
             out=w1_raw[:].bitcast(I32), in_=w1t_words.rearrange("e s p b -> p (e s) b").bitcast(I32)
         )
@@ -88,6 +91,7 @@ def tile_moe_sdb_silu_kernel(
                 out=w1s_raw[32 * q : 32 * q + 4, :, :].bitcast(I32),
                 in_=w1t_scales[:, 0, 4 * q : 4 * q + 4, :].rearrange("e r k -> r e k").bitcast(I32),
             )
+        nc.sync.dma_start(out=g_rest[:], in_=gate[:, C:T])
 
         for q in range(4):
             rows = slice(32 * q, 32 * q + 4 * PASSES)
@@ -101,32 +105,24 @@ def tile_moe_sdb_silu_kernel(
                 out=w2_codes[s][:].rearrange("p (t m) -> p m t", t=PACK),
                 in_=w2_raw[s][:].rearrange("p (m t) -> p m t", t=PACK),
             )
-        for e in range(E):
-            nc.scalar.activation(sig[e][:], pre[e][:].rearrange("p j c -> p (j c)"), ACT.Sigmoid)
+        nc.vector.tensor_scalar(minus_g_first[:], g_first[:], -1.0, None, ALU.mult)
+        for e, lo, hi in ((0, 0, 4 * C), (1, 0, 4 * C), (2, 0, 2 * C), (2, 2 * C, 4 * C)):
+            nc.scalar.activation(sig[e][:, lo:hi], pre[e][:].rearrange("p j c -> p (j c)")[:, lo:hi], ACT.Sigmoid)
         for e in range(E):
             nc.scalar.activation(neg_silu[e], pre[e][:].rearrange("p j c -> p (j c)"), ACT.Silu, scale=-1.0)
 
-        gated = [tile([P, PACK, C], F32, f"gated{e}") for e in range(E - 1)]
-        for e in range(E):
-            nc.gpsimd.tensor_scalar(minus_g[e][:], g[e][:], -1.0, 0.0, ALU.mult, ALU.add)
-            for t in range(PACK if e < E - 1 else 0):
-                nc.gpsimd.tensor_tensor(gated[e][:, t, :], sig[e][:, t * C : (t + 1) * C], minus_g[e][:], ALU.mult)
+        first_picked = tile([P, PACK * C], F32, "first_picked")
+        picked = [x[:].rearrange("p (t c) -> p t c", t=PACK) for x in [first_picked] + sig[:-1]]
 
-        first_picked = tile([P, PACK, C], F32, "first_picked")
-        picked = [first_picked, pre[2], first_picked]
+        minus_g = [minus_g_first[:]]
 
         def gather(e, t):
             window = dc[t][:].indirect(offsets[:, e * OFFS_COLS : (e + 1) * OFFS_COLS])
-            if e == 1:
-                nc.scalar.activation(picked[e][:, t, :], window, ACT.Copy)
-            elif e == 0:
-                nc.vector.tensor_copy(picked[e][:, t, :], window)
-            else:
-                nc.vector.tensor_tensor(picked[e][:, t, :], window, minus_g[e][:], ALU.mult)
+            nc.vector.tensor_tensor(picked[e][:, t, :], window, minus_g[e], ALU.mult)
 
         banks = [[ps.tile([P, BANK], F32, name="bank") for cut in TOKEN_CUTS] for t in range(PACK)]
-        for s in range(PASSES):
-            for t in range(PACK):
+        for t in range(PACK):
+            for s in range(PASSES):
                 for bank, (lo, hi) in zip(banks[t], TOKEN_CUTS):
                     nc.tensor.matmul_mx(
                         out=bank[:, : hi - lo],
@@ -137,38 +133,42 @@ def tile_moe_sdb_silu_kernel(
                         start=(s == 0),
                         stop=(s == PASSES - 1),
                     )
-        for t in range(PACK):
             for bank, (lo, hi) in zip(banks[t], TOKEN_CUTS):
                 nc.vector.tensor_copy(out=dc[t][:, lo:hi], in_=bank[:, : hi - lo])
             gather(0, t)
 
-        nc.vector.tensor_copy(
+        nc.scalar.copy(
             out=w1_codes[:].bitcast(U16).rearrange("p t m -> p m t"),
             in_=w1_raw[:].bitcast(U16).rearrange("p e (m t) -> p (e m) t", t=PACK),
         )
-        nc.vector.tensor_copy(
-            out=w1_scale[:].rearrange("p t m -> p m t"),
-            in_=w1s_raw[:].rearrange("p e (m t) -> p (e m) t", t=PACK),
-        )
+        w1_scale = tile([P, PACK, E * P], U8, "w1_scale", tag="pre0")
 
         dx = [[tile([P, 2, C], F32, f"dx{e}_{h}") for h in range(2)] for e in range(E)]
 
         def expert(e):
-            minus_d = tile([P, PACK, C], F32, f"minus_d{e}")
-            factor = gated[e][:].rearrange("p j c -> p (j c)") if e < E - 1 else sig[e][:]
+            minus_d = tile([P, PACK, C], F32, f"minus_d{e}", tag=f"da{e - 1}")
             nc.vector.scalar_tensor_tensor(
-                minus_d[:].rearrange("p j c -> p (j c)"), neg_silu[e], 1.0, factor, ALU.subtract, ALU.mult
+                minus_d[:].rearrange("p j c -> p (j c)"), neg_silu[e], 1.0, sig[e][:], ALU.subtract, ALU.mult
             )
-            if e > 0:
+            if e == 0:
+                nc.vector.tensor_copy(
+                    out=w1_scale[:].rearrange("p t m -> p m t"),
+                    in_=w1s_raw[:].rearrange("p e (m t) -> p (e m) t", t=PACK),
+                )
+            else:
                 for t in range(PACK):
                     gather(e, t)
             da = tile([P, C, PACK], BF16, f"da{e}")
             nc.vector.tensor_tensor(
                 da[:].rearrange("p (c i) t -> p c t i", i=4),
-                picked[e][:].rearrange("p t (c i) -> p c t i", i=4),
+                picked[e].rearrange("p t (c i) -> p c t i", i=4),
                 minus_d[:].rearrange("p t (c i) -> p c t i", i=4),
                 ALU.mult,
             )
+            if e == 0:
+                minus_g_rest = tile([P, T - C], F32, "minus_g_rest", tag="da-1")
+                nc.vector.tensor_scalar(minus_g_rest[:], g_rest[:], -1.0, None, ALU.mult)
+                minus_g.extend([minus_g_rest[:, 0:C], minus_g_rest[:, C : 2 * C]])
             da_codes = tile([P, C], I32, f"da_codes{e}")
             da_scale = tile([P, C], U8, f"da_scale{e}")
             nc.vector.quantize_mx(
@@ -187,7 +187,7 @@ def tile_moe_sdb_silu_kernel(
                         start=True,
                         stop=True,
                     )
-                if e > 0 and h == 0:
+                if e == E - 1:
                     nc.vector.tensor_copy(out=dx[e][h][:].rearrange("p u c -> p (u c)"), in_=bank[:])
                 else:
                     nc.scalar.copy(out=dx[e][h][:].rearrange("p u c -> p (u c)"), in_=bank[:])
@@ -204,9 +204,10 @@ def tile_moe_sdb_silu_kernel(
             scatter(0, t, False)
         expert(1)
         expert(2)
-        for e in (1, 2):
-            for t in range(PACK):
-                scatter(e, t, t % 2 == 0)
+        for t in range(PACK):
+            scatter(1, t, t == 0)
+        for t in range(PACK):
+            scatter(2, t, t % 2 == 0)
 
         out_rows = out_0.rearrange("(p j) c -> p j c", j=PACK)
         pairs = tile([P, 2, T, 2], BF16, "pairs")
@@ -217,10 +218,11 @@ def tile_moe_sdb_silu_kernel(
         y_scale = tile([P, T], U8, "y_scale")
         out_words = out_1[0].rearrange("p c d -> p (c d)").bitcast(I32)
         for lo, hi in TOKEN_CUTS:
-            woven = tile([P, hi - lo, 2], I32, f"woven{lo}")
-            nc.vector.tensor_copy(
+            woven = tile([P, hi - lo, 2], U32, f"woven{lo}")
+            weave = nc.vector.tensor_copy if lo == 0 else nc.scalar.copy
+            weave(
                 out=woven[:],
-                in_=pairs[:].rearrange("p h c u -> p h (c u)").bitcast(I32)[:, :, lo:hi].rearrange("p h c -> p c h"),
+                in_=pairs[:].rearrange("p h c u -> p h (c u)").bitcast(U32)[:, :, lo:hi].rearrange("p h c -> p c h"),
             )
             nc.vector.quantize_mx(
                 out=y_codes[:, lo:hi].bitcast(FP8X4),

@@ -143,7 +143,12 @@ def tile_moe_sdb_silu_kernel(
         )
         w1_scale = tile([P, PACK, E * P], U8, "w1_scale", tag="pre0")
 
-        dx = [[tile([P, 2, C], F32, f"dx{e}_{h}") for h in range(2)] for e in range(E)]
+        dx = {}
+        sums = {}
+
+        def empty_bank(e, h, copy, tag=None):
+            dx[e, h] = tile([P, 2, C], F32, f"dx{e}_{h}", tag=tag)
+            copy(out=dx[e, h][:].rearrange("p u c -> p (u c)"), in_=sums[e, h][:])
 
         def expert(e):
             minus_d = tile([P, PACK, C], F32, f"minus_d{e}", tag=f"da{e - 1}")
@@ -187,31 +192,36 @@ def tile_moe_sdb_silu_kernel(
                         start=True,
                         stop=True,
                     )
-                if e == E - 1:
-                    nc.vector.tensor_copy(out=dx[e][h][:].rearrange("p u c -> p (u c)"), in_=bank[:])
-                else:
-                    nc.scalar.copy(out=dx[e][h][:].rearrange("p u c -> p (u c)"), in_=bank[:])
+                sums[e, h] = bank
 
-        def scatter(e, t, on_vector):
-            window = y[t][:].indirect(offsets[:, e * OFFS_COLS : (e + 1) * OFFS_COLS])
+        def scatter(e, t, on_vector, lo=0, hi=C):
+            window = y[t][:].indirect(offsets[:, (e * C + lo) // 16 : (e * C + hi) // 16])
             if on_vector:
-                nc.vector.tensor_copy(window, dx[e][t % 2][:, t // 2, :])
+                nc.vector.tensor_copy(window, dx[e, t % 2][:, t // 2, lo:hi])
             else:
-                nc.scalar.activation(window, dx[e][t % 2][:, t // 2, :], ACT.Copy)
+                nc.scalar.activation(window, dx[e, t % 2][:, t // 2, lo:hi], ACT.Copy)
 
         expert(0)
+        for h in range(2):
+            empty_bank(0, h, nc.scalar.copy)
         for t in range(PACK):
             scatter(0, t, False)
         expert(1)
+        empty_bank(1, 1, nc.scalar.copy)
+        scatter(1, 1, False)
+        scatter(1, 3, False)
         expert(2)
-        for t in range(PACK):
-            scatter(1, t, t == 0)
+        empty_bank(1, 0, nc.vector.tensor_copy, tag="sig1")
+        scatter(1, 0, True)
+        scatter(1, 2, False)
+        empty_bank(2, 0, nc.vector.tensor_copy)
+        empty_bank(2, 1, nc.scalar.copy)
         for t in range(PACK):
             scatter(2, t, t % 2 == 0)
 
         out_rows = out_0.rearrange("(p j) c -> p j c", j=PACK)
-        pairs = tile([P, 2, T, 2], BF16, "pairs")
-        for t in range(PACK):
+        pairs = tile([P, 2, T, 2], BF16, "pairs", tag="dx2_0")
+        for t in (0, 2, 1, 3):
             nc.sync.dma_start(out=out_rows[:, t, :], in_=y[t][:])
             nc.vector.tensor_copy(out=pairs[:, t // 2, :, t % 2], in_=y[t][:])
         y_codes = tile([P, T], I32, "y_codes")

@@ -8,7 +8,6 @@ FLOPS = 2 * N * H * T + 2 * H * K * E * C
 F32 = mybir.dt.float32
 BF16 = mybir.dt.bfloat16
 I32 = mybir.dt.int32
-U32 = mybir.dt.uint32
 U16 = mybir.dt.uint16
 U8 = mybir.dt.uint8
 FP8X4 = mybir.dt.float8_e4m3fn_x4
@@ -19,9 +18,12 @@ ACT = mybir.ActivationFunctionType
 P = 128
 PACK = 4
 PASSES = N // (P * PACK)
+QUADRANTS = 4
 BANK = 512
-TOKEN_CUTS = ((0, 512), (512, 768))
+BANKS = 8
+TOKEN_CUTS = ((0, BANK), (BANK, T))
 OFFS_COLS = C // 16
+RUN = 4
 
 
 def tile_moe_sdb_silu_kernel(
@@ -30,7 +32,7 @@ def tile_moe_sdb_silu_kernel(
     nc = tc.nc
     with ExitStack() as ctx:
         sb = ctx.enter_context(tc.tile_pool(name="sb", bufs=1))
-        ps = ctx.enter_context(tc.psum_pool(name="ps", bufs=8))
+        ps = ctx.enter_context(tc.psum_pool(name="ps", bufs=BANKS))
 
         def tile(shape, dtype, name, tag=None):
             return sb.tile(shape, dtype, name=name, tag=tag or name, align_bytes=64)
@@ -48,7 +50,7 @@ def tile_moe_sdb_silu_kernel(
         w1s_raw = tile([P, E, K], U8, "w1s_raw")
         pre = [tile([P, PACK, C], F32, f"pre{e}") for e in range(E)]
         sig = [tile([P, PACK * C], F32, f"sig{e}") for e in range(E)]
-        neg_silu = [tile([P, PACK * C], F32, f"neg_silu{e}")[:] for e in range(E)]
+        neg_silu = [tile([P, PACK * C], F32, f"neg_silu{e}") for e in range(E)]
         g_first = tile([P, C], F32, "g_first")
         g_rest = tile([P, T - C], F32, "g_rest")
         minus_g_first = tile([P, C], F32, "minus_g_first")
@@ -59,7 +61,7 @@ def tile_moe_sdb_silu_kernel(
         nc.gpsimd.memset(dy_scale[:].bitcast(I32), 0)
         nc.gpsimd.memset(w1s_raw[:].rearrange("p e k -> p (e k)").bitcast(I32), 0)
 
-        for q in range(4):
+        for q in range(QUADRANTS):
             nc.sync.dma_start(
                 out=w2s_rows[32 * q : 32 * q + 4 * PASSES, :].bitcast(I32),
                 in_=w2t_scales[:, 4 * q : 4 * q + 4, :].bitcast(I32),
@@ -70,30 +72,30 @@ def tile_moe_sdb_silu_kernel(
             nc.sync.dma_start(out=dy_codes[s][:], in_=dy_words[s].rearrange("p n d -> p (n d)").bitcast(I32))
 
         load_pass(0)
-        for q in range(4):
+        for q in range(QUADRANTS):
             nc.sync.dma_start(
                 out=dy_scale[32 * q : 32 * q + 4 * PASSES, :].bitcast(I32),
                 in_=dy_scales[:, 4 * q : 4 * q + 4, :].bitcast(I32),
             )
         load_pass(1)
         nc.sync.dma_start(offsets[:], offs)
-        a_rows = a.rearrange("(p j) c -> p j c", j=PACK)
+        a_rows = a.rearrange("(p t) c -> p t c", t=PACK)
         nc.sync.dma_start(out=pre[0][:], in_=a_rows[:, :, 0:C])
         nc.sync.dma_start(out=g_first[:], in_=gate[:, 0:C])
         nc.sync.dma_start(out=pre[1][:], in_=a_rows[:, :, C : 2 * C])
-        for j in (0, 2):
-            nc.sync.dma_start(out=pre[2][:, j : j + 2, :], in_=a_rows[:, j : j + 2, 2 * C : 3 * C])
+        for t in (0, 2):
+            nc.sync.dma_start(out=pre[2][:, t : t + 2, :], in_=a_rows[:, t : t + 2, 2 * C : 3 * C])
         nc.sync.dma_start(
             out=w1_raw[:].bitcast(I32), in_=w1t_words.rearrange("e s p b -> p (e s) b").bitcast(I32)
         )
-        for q in range(4):
+        for q in range(QUADRANTS):
             nc.sync.dma_start(
                 out=w1s_raw[32 * q : 32 * q + 4, :, :].bitcast(I32),
                 in_=w1t_scales[:, 0, 4 * q : 4 * q + 4, :].rearrange("e r k -> r e k").bitcast(I32),
             )
         nc.sync.dma_start(out=g_rest[:], in_=gate[:, C:T])
 
-        for q in range(4):
+        for q in range(QUADRANTS):
             rows = slice(32 * q, 32 * q + 4 * PASSES)
             nc.vector.tensor_copy(out=w2s_raw[rows, :].bitcast(I32), in_=w2s_rows[rows, :].bitcast(I32))
         nc.vector.tensor_copy(
@@ -105,20 +107,22 @@ def tile_moe_sdb_silu_kernel(
                 out=w2_codes[s][:].rearrange("p (t m) -> p m t", t=PACK),
                 in_=w2_raw[s][:].rearrange("p (m t) -> p m t", t=PACK),
             )
+
         nc.vector.tensor_scalar(minus_g_first[:], g_first[:], -1.0, None, ALU.mult)
         for e, lo, hi in ((0, 0, 4 * C), (1, 0, 4 * C), (2, 0, 2 * C), (2, 2 * C, 4 * C)):
-            nc.scalar.activation(sig[e][:, lo:hi], pre[e][:].rearrange("p j c -> p (j c)")[:, lo:hi], ACT.Sigmoid)
+            nc.scalar.activation(sig[e][:, lo:hi], pre[e][:].rearrange("p t c -> p (t c)")[:, lo:hi], ACT.Sigmoid)
         for e in range(E):
-            nc.scalar.activation(neg_silu[e], pre[e][:].rearrange("p j c -> p (j c)"), ACT.Silu, scale=-1.0)
+            nc.scalar.activation(neg_silu[e][:], pre[e][:].rearrange("p t c -> p (t c)"), ACT.Silu, scale=-1.0)
 
         first_picked = tile([P, PACK * C], F32, "first_picked")
         picked = [x[:].rearrange("p (t c) -> p t c", t=PACK) for x in [first_picked] + sig[:-1]]
-
         minus_g = [minus_g_first[:]]
 
+        def slots(e):
+            return offsets[:, e * OFFS_COLS : (e + 1) * OFFS_COLS]
+
         def gather(e, t):
-            window = dc[t][:].indirect(offsets[:, e * OFFS_COLS : (e + 1) * OFFS_COLS])
-            nc.vector.tensor_tensor(picked[e][:, t, :], window, minus_g[e], ALU.mult)
+            nc.vector.tensor_tensor(picked[e][:, t, :], dc[t][:].indirect(slots(e)), minus_g[e], ALU.mult)
 
         banks = [[ps.tile([P, BANK], F32, name="bank") for cut in TOKEN_CUTS] for t in range(PACK)]
         for t in range(PACK):
@@ -143,17 +147,13 @@ def tile_moe_sdb_silu_kernel(
         )
         w1_scale = tile([P, PACK, E * P], U8, "w1_scale", tag="pre0")
 
-        dx = {}
         sums = {}
-
-        def empty_bank(e, h, copy, tag=None):
-            dx[e, h] = tile([P, 2, C], F32, f"dx{e}_{h}", tag=tag)
-            copy(out=dx[e, h][:].rearrange("p u c -> p (u c)"), in_=sums[e, h][:])
+        dx = {}
 
         def expert(e):
-            minus_d = tile([P, PACK, C], F32, f"minus_d{e}", tag=f"da{e - 1}")
+            minus_d = tile([P, PACK, C], F32, f"minus_d{e}", tag=f"da{e - 1}" if e > 0 else "minus_d0")
             nc.vector.scalar_tensor_tensor(
-                minus_d[:].rearrange("p j c -> p (j c)"), neg_silu[e], 1.0, sig[e][:], ALU.subtract, ALU.mult
+                minus_d[:].rearrange("p t c -> p (t c)"), neg_silu[e][:], 1.0, sig[e][:], ALU.subtract, ALU.mult
             )
             if e == 0:
                 nc.vector.tensor_copy(
@@ -165,13 +165,13 @@ def tile_moe_sdb_silu_kernel(
                     gather(e, t)
             da = tile([P, C, PACK], BF16, f"da{e}")
             nc.vector.tensor_tensor(
-                da[:].rearrange("p (c i) t -> p c t i", i=4),
-                picked[e].rearrange("p t (c i) -> p c t i", i=4),
-                minus_d[:].rearrange("p t (c i) -> p c t i", i=4),
+                da[:].rearrange("p (c i) t -> p c t i", i=RUN),
+                picked[e].rearrange("p t (c i) -> p c t i", i=RUN),
+                minus_d[:].rearrange("p t (c i) -> p c t i", i=RUN),
                 ALU.mult,
             )
             if e == 0:
-                minus_g_rest = tile([P, T - C], F32, "minus_g_rest", tag="da-1")
+                minus_g_rest = tile([P, T - C], F32, "minus_g_rest", tag="minus_d0")
                 nc.vector.tensor_scalar(minus_g_rest[:], g_rest[:], -1.0, None, ALU.mult)
                 minus_g.extend([minus_g_rest[:, 0:C], minus_g_rest[:, C : 2 * C]])
             da_codes = tile([P, C], I32, f"da_codes{e}")
@@ -180,11 +180,11 @@ def tile_moe_sdb_silu_kernel(
                 out=da_codes[:].bitcast(FP8X4), scales=da_scale[:], in_=da[:].rearrange("p c t -> p (c t)")
             )
             for h in range(2):
-                bank = ps.tile([P, BANK], F32, name="bank")
+                sums[e, h] = ps.tile([P, BANK], F32, name="bank")
                 for u in range(2):
                     t = h + 2 * u
                     nc.tensor.matmul_mx(
-                        out=bank[:, u * C : (u + 1) * C],
+                        out=sums[e, h][:, u * C : (u + 1) * C],
                         lhsT=w1_codes[:, t, 2 * e * P : 2 * (e + 1) * P].bitcast(FP4X4),
                         lhsT_scale=w1_scale[:, t, e * P : (e + 1) * P],
                         rhs=da_codes[:].bitcast(FP8X4),
@@ -192,55 +192,58 @@ def tile_moe_sdb_silu_kernel(
                         start=True,
                         stop=True,
                     )
-                sums[e, h] = bank
 
-        def scatter(e, t, on_vector, lo=0, hi=C):
-            window = y[t][:].indirect(offsets[:, (e * C + lo) // 16 : (e * C + hi) // 16])
-            if on_vector:
-                nc.vector.tensor_copy(window, dx[e, t % 2][:, t // 2, lo:hi])
-            else:
-                nc.scalar.activation(window, dx[e, t % 2][:, t // 2, lo:hi], ACT.Copy)
+        def empty_bank(e, h, copy, tag=None):
+            dx[e, h] = tile([P, 2, C], F32, f"dx{e}_{h}", tag=tag)
+            copy(out=dx[e, h][:].rearrange("p u c -> p (u c)"), in_=sums[e, h][:])
+
+        def scatter_on_vector(e, t):
+            nc.vector.tensor_copy(y[t][:].indirect(slots(e)), dx[e, t % 2][:, t // 2, :])
+
+        def scatter_on_scalar(e, t):
+            nc.scalar.activation(y[t][:].indirect(slots(e)), dx[e, t % 2][:, t // 2, :], ACT.Copy)
 
         expert(0)
         for h in range(2):
             empty_bank(0, h, nc.scalar.copy)
         for t in range(PACK):
-            scatter(0, t, False)
+            scatter_on_scalar(0, t)
         expert(1)
         empty_bank(1, 1, nc.scalar.copy)
-        scatter(1, 1, False)
-        scatter(1, 3, False)
+        scatter_on_scalar(1, 1)
+        scatter_on_scalar(1, 3)
         expert(2)
         empty_bank(1, 0, nc.vector.tensor_copy, tag="sig1")
-        scatter(1, 0, True)
-        scatter(1, 2, False)
+        scatter_on_vector(1, 0)
+        scatter_on_scalar(1, 2)
         empty_bank(2, 0, nc.vector.tensor_copy)
         empty_bank(2, 1, nc.scalar.copy)
         for t in range(PACK):
-            scatter(2, t, t % 2 == 0)
+            scatter = scatter_on_vector if t % 2 == 0 else scatter_on_scalar
+            scatter(2, t)
 
-        out_rows = out_0.rearrange("(p j) c -> p j c", j=PACK)
-        pairs = tile([P, 2, T, 2], BF16, "pairs", tag="dx2_0")
+        out_rows = out_0.rearrange("(p t) c -> p t c", t=PACK)
+        rounded = tile([P, PACK, T], BF16, "rounded", tag="dx2_0")
         for t in (0, 2, 1, 3):
             nc.sync.dma_start(out=out_rows[:, t, :], in_=y[t][:])
-            nc.vector.tensor_copy(out=pairs[:, t // 2, :, t % 2], in_=y[t][:])
+            nc.vector.tensor_copy(out=rounded[:, t, :], in_=y[t][:])
         y_codes = tile([P, T], I32, "y_codes")
         y_scale = tile([P, T], U8, "y_scale")
         out_words = out_1[0].rearrange("p c d -> p (c d)").bitcast(I32)
-        for lo, hi in TOKEN_CUTS:
-            woven = tile([P, hi - lo, 2], U32, f"woven{lo}")
-            weave = nc.vector.tensor_copy if lo == 0 else nc.scalar.copy
+        for (lo, hi), weave in zip(TOKEN_CUTS, (nc.vector.tensor_copy, nc.scalar.copy)):
+            woven = tile([P, hi - lo, PACK], BF16, f"woven{lo}")
             weave(
-                out=woven[:],
-                in_=pairs[:].rearrange("p h c u -> p h (c u)").bitcast(U32)[:, :, lo:hi].rearrange("p h c -> p c h"),
+                out=woven[:].rearrange("p (c i) t -> p c t i", i=RUN),
+                in_=rounded[:, :, lo:hi].rearrange("p t (c i) -> p c t i", i=RUN),
             )
             nc.vector.quantize_mx(
                 out=y_codes[:, lo:hi].bitcast(FP8X4),
                 scales=y_scale[:, lo:hi],
-                in_=woven[:].rearrange("p c h -> p (c h)").bitcast(BF16),
+                in_=woven[:].rearrange("p c t -> p (c t)"),
             )
             nc.sync.dma_start(out=out_words[:, lo:hi], in_=y_codes[:, lo:hi])
-        for q in range(4):
-            nc.scalar.dma_start(
+        for q in range(QUADRANTS):
+            queue = nc.scalar if q < QUADRANTS - 1 else nc.sync
+            queue.dma_start(
                 out=out_2[0, 4 * q : 4 * q + 4, :].bitcast(I32), in_=y_scale[32 * q : 32 * q + 4, :].bitcast(I32)
             )

from contextlib import ExitStack

import concourse.mybir as mybir

K, T, E, C, H, N = 512, 768, 3, 256, 512, 1024
FLOPS = 2 * N * H * T + 2 * H * K * E * C

F32 = mybir.dt.float32
BF16 = mybir.dt.bfloat16
I32 = mybir.dt.int32
U16 = mybir.dt.uint16
U8 = mybir.dt.uint8
FP8X4 = mybir.dt.float8_e4m3fn_x4
FP4X4 = mybir.dt.float4_e2m1fn_x4
ALU = mybir.AluOpType
ACT = mybir.ActivationFunctionType

P = 128
PACK = 4
PASSES = N // (P * PACK)
QUADRANTS = 4
BANK = 512
BANKS = 8
TOKEN_CUTS = ((0, BANK), (BANK, T))
OFFS_COLS = C // 16
RUN = 4


def tile_moe_sdb_silu_kernel(
    tc, dy_words, dy_scales, w2t_words, w2t_scales, w1t_words, w1t_scales, a, gate, offs, out_0, out_1, out_2
):
    nc = tc.nc
    with ExitStack() as ctx:
        sb = ctx.enter_context(tc.tile_pool(name="sb", bufs=1))
        ps = ctx.enter_context(tc.psum_pool(name="ps", bufs=BANKS))

        def tile(shape, dtype, name, tag=None):
            return sb.tile(shape, dtype, name=name, tag=tag or name, align_bytes=64)

        offsets = sb.tile([P, T // 16], U16, name="offsets")
        w2_raw = [tile([P, H], I32, f"w2_raw{s}") for s in range(PASSES)]
        w2_codes = [tile([P, H], I32, f"w2_codes{s}") for s in range(PASSES)]
        w2s_rows = tile([P, H], U8, "w2s_rows")
        w2s_raw = tile([P, H], U8, "w2s_raw")
        w2_scale = tile([P, H], U8, "w2_scale")
        dy_codes = [tile([P, T], I32, f"dy_codes{s}") for s in range(PASSES)]
        dy_scale = tile([P, T], U8, "dy_scale")
        w1_raw = tile([P, E, 2 * K], U8, "w1_raw")
        w1_codes = tile([P, PACK, 2 * E * P], U8, "w1_codes")
        w1s_raw = tile([P, E, K], U8, "w1s_raw")
        pre = [tile([P, PACK, C], F32, f"pre{e}") for e in range(E)]
        sig = [tile([P, PACK * C], F32, f"sig{e}") for e in range(E)]
        neg_silu = [tile([P, PACK * C], F32, f"neg_silu{e}") for e in range(E)]
        g_first = tile([P, C], F32, "g_first")
        g_rest = tile([P, T - C], F32, "g_rest")
        minus_g_first = tile([P, C], F32, "minus_g_first")
        dc = [tile([P, T], F32, f"dc{t}") for t in range(PACK)]
        y = [tile([P, T], F32, f"y{t}") for t in range(PACK)]

        nc.vector.memset(w2s_raw[:].bitcast(I32), 0)
        nc.gpsimd.memset(dy_scale[:].bitcast(I32), 0)
        nc.gpsimd.memset(w1s_raw[:].rearrange("p e k -> p (e k)").bitcast(I32), 0)

        for q in range(QUADRANTS):
            nc.sync.dma_start(
                out=w2s_rows[32 * q : 32 * q + 4 * PASSES, :].bitcast(I32),
                in_=w2t_scales[:, 4 * q : 4 * q + 4, :].bitcast(I32),
            )

        def load_pass(s):
            nc.sync.dma_start(out=w2_raw[s][:], in_=w2t_words[s].rearrange("p n d -> p (n d)").bitcast(I32))
            nc.sync.dma_start(out=dy_codes[s][:], in_=dy_words[s].rearrange("p n d -> p (n d)").bitcast(I32))

        load_pass(0)
        for q in range(QUADRANTS):
            nc.sync.dma_start(
                out=dy_scale[32 * q : 32 * q + 4 * PASSES, :].bitcast(I32),
                in_=dy_scales[:, 4 * q : 4 * q + 4, :].bitcast(I32),
            )
        load_pass(1)
        nc.sync.dma_start(offsets[:], offs)
        a_rows = a.rearrange("(p t) c -> p t c", t=PACK)
        nc.sync.dma_start(out=pre[0][:], in_=a_rows[:, :, 0:C])
        nc.sync.dma_start(out=g_first[:], in_=gate[:, 0:C])
        nc.sync.dma_start(out=pre[1][:], in_=a_rows[:, :, C : 2 * C])
        for t in (0, 2):
            nc.sync.dma_start(out=pre[2][:, t : t + 2, :], in_=a_rows[:, t : t + 2, 2 * C : 3 * C])
        nc.sync.dma_start(
            out=w1_raw[:].bitcast(I32), in_=w1t_words.rearrange("e s p b -> p (e s) b").bitcast(I32)
        )
        for q in range(QUADRANTS):
            nc.sync.dma_start(
                out=w1s_raw[32 * q : 32 * q + 4, :, :].bitcast(I32),
                in_=w1t_scales[:, 0, 4 * q : 4 * q + 4, :].rearrange("e r k -> r e k").bitcast(I32),
            )
        nc.sync.dma_start(out=g_rest[:], in_=gate[:, C:T])

        for q in range(QUADRANTS):
            rows = slice(32 * q, 32 * q + 4 * PASSES)
            nc.vector.tensor_copy(out=w2s_raw[rows, :].bitcast(I32), in_=w2s_rows[rows, :].bitcast(I32))
        nc.vector.tensor_copy(
            out=w2_scale[:].rearrange("p (t m) -> p m t", t=PACK),
            in_=w2s_raw[:].rearrange("p (m t) -> p m t", t=PACK),
        )
        for s in range(PASSES):
            nc.vector.tensor_copy(
                out=w2_codes[s][:].rearrange("p (t m) -> p m t", t=PACK),
                in_=w2_raw[s][:].rearrange("p (m t) -> p m t", t=PACK),
            )

        nc.vector.tensor_scalar(minus_g_first[:], g_first[:], -1.0, None, ALU.mult)
        for e, lo, hi in ((0, 0, 4 * C), (1, 0, 4 * C), (2, 0, 2 * C), (2, 2 * C, 4 * C)):
            nc.scalar.activation(sig[e][:, lo:hi], pre[e][:].rearrange("p t c -> p (t c)")[:, lo:hi], ACT.Sigmoid)
        for e in range(E):
            nc.scalar.activation(neg_silu[e][:], pre[e][:].rearrange("p t c -> p (t c)"), ACT.Silu, scale=-1.0)

        first_picked = tile([P, PACK * C], F32, "first_picked")
        picked = [x[:].rearrange("p (t c) -> p t c", t=PACK) for x in [first_picked] + sig[:-1]]
        minus_g = [minus_g_first[:]]

        def slots(e):
            return offsets[:, e * OFFS_COLS : (e + 1) * OFFS_COLS]

        def gather(e, t):
            nc.vector.tensor_tensor(picked[e][:, t, :], dc[t][:].indirect(slots(e)), minus_g[e], ALU.mult)

        banks = [[ps.tile([P, BANK], F32, name="bank") for cut in TOKEN_CUTS] for t in range(PACK)]
        for t in range(PACK):
            for s in range(PASSES):
                for bank, (lo, hi) in zip(banks[t], TOKEN_CUTS):
                    nc.tensor.matmul_mx(
                        out=bank[:, : hi - lo],
                        lhsT=w2_codes[s][:, t * P : (t + 1) * P].bitcast(FP8X4),
                        lhsT_scale=w2_scale[4 * s :, t * P : (t + 1) * P],
                        rhs=dy_codes[s][:, lo:hi].bitcast(FP8X4),
                        rhs_scale=dy_scale[4 * s :, lo:hi],
                        start=(s == 0),
                        stop=(s == PASSES - 1),
                    )
            for bank, (lo, hi) in zip(banks[t], TOKEN_CUTS):
                nc.vector.tensor_copy(out=dc[t][:, lo:hi], in_=bank[:, : hi - lo])
            gather(0, t)

        nc.scalar.copy(
            out=w1_codes[:].bitcast(U16).rearrange("p t m -> p m t"),
            in_=w1_raw[:].bitcast(U16).rearrange("p e (m t) -> p (e m) t", t=PACK),
        )
        w1_scale = tile([P, PACK, E * P], U8, "w1_scale", tag="pre0")

        sums = {}
        dx = {}

        def expert(e):
            minus_d = tile([P, PACK, C], F32, f"minus_d{e}", tag=f"da{e - 1}" if e > 0 else "minus_d0")
            nc.vector.scalar_tensor_tensor(
                minus_d[:].rearrange("p t c -> p (t c)"), neg_silu[e][:], 1.0, sig[e][:], ALU.subtract, ALU.mult
            )
            if e == 0:
                nc.vector.tensor_copy(
                    out=w1_scale[:].rearrange("p t m -> p m t"),
                    in_=w1s_raw[:].rearrange("p e (m t) -> p (e m) t", t=PACK),
                )
            else:
                for t in range(PACK):
                    gather(e, t)
            da = tile([P, C, PACK], BF16, f"da{e}")
            nc.vector.tensor_tensor(
                da[:].rearrange("p (c i) t -> p c t i", i=RUN),
                picked[e].rearrange("p t (c i) -> p c t i", i=RUN),
                minus_d[:].rearrange("p t (c i) -> p c t i", i=RUN),
                ALU.mult,
            )
            if e == 0:
                minus_g_rest = tile([P, T - C], F32, "minus_g_rest", tag="minus_d0")
                nc.vector.tensor_scalar(minus_g_rest[:], g_rest[:], -1.0, None, ALU.mult)
                minus_g.extend([minus_g_rest[:, 0:C], minus_g_rest[:, C : 2 * C]])
            da_codes = tile([P, C], I32, f"da_codes{e}")
            da_scale = tile([P, C], U8, f"da_scale{e}")
            nc.vector.quantize_mx(
                out=da_codes[:].bitcast(FP8X4), scales=da_scale[:], in_=da[:].rearrange("p c t -> p (c t)")
            )
            for h in range(2):
                sums[e, h] = ps.tile([P, BANK], F32, name="bank")
                for u in range(2):
                    t = h + 2 * u
                    nc.tensor.matmul_mx(
                        out=sums[e, h][:, u * C : (u + 1) * C],
                        lhsT=w1_codes[:, t, 2 * e * P : 2 * (e + 1) * P].bitcast(FP4X4),
                        lhsT_scale=w1_scale[:, t, e * P : (e + 1) * P],
                        rhs=da_codes[:].bitcast(FP8X4),
                        rhs_scale=da_scale[:],
                        start=True,
                        stop=True,
                    )

        def empty_bank(e, h, copy, tag=None):
            dx[e, h] = tile([P, 2, C], F32, f"dx{e}_{h}", tag=tag)
            copy(out=dx[e, h][:].rearrange("p u c -> p (u c)"), in_=sums[e, h][:])

        def scatter_on_vector(e, t):
            nc.vector.tensor_copy(y[t][:].indirect(slots(e)), dx[e, t % 2][:, t // 2, :])

        def scatter_on_scalar(e, t):
            nc.scalar.activation(y[t][:].indirect(slots(e)), dx[e, t % 2][:, t // 2, :], ACT.Copy)

        expert(0)
        for h in range(2):
            empty_bank(0, h, nc.scalar.copy)
        for t in range(PACK):
            scatter_on_scalar(0, t)
        expert(1)
        empty_bank(1, 1, nc.scalar.copy)
        scatter_on_scalar(1, 1)
        scatter_on_scalar(1, 3)
        expert(2)
        empty_bank(1, 0, nc.vector.tensor_copy, tag="sig1")
        scatter_on_vector(1, 0)
        scatter_on_scalar(1, 2)
        empty_bank(2, 0, nc.vector.tensor_copy)
        empty_bank(2, 1, nc.scalar.copy)
        for t in range(PACK):
            scatter = scatter_on_vector if t % 2 == 0 else scatter_on_scalar
            scatter(2, t)

        out_rows = out_0.rearrange("(p t) c -> p t c", t=PACK)
        rounded = tile([P, PACK, T], BF16, "rounded", tag="dx2_0")
        for t in (0, 2, 1, 3):
            nc.sync.dma_start(out=out_rows[:, t, :], in_=y[t][:])
            nc.vector.tensor_copy(out=rounded[:, t, :], in_=y[t][:])
        y_codes = tile([P, T], I32, "y_codes")
        y_scale = tile([P, T], U8, "y_scale")
        out_words = out_1[0].rearrange("p c d -> p (c d)").bitcast(I32)
        for (lo, hi), weave in zip(TOKEN_CUTS, (nc.vector.tensor_copy, nc.scalar.copy)):
            woven = tile([P, hi - lo, PACK], BF16, f"woven{lo}")
            weave(
                out=woven[:].rearrange("p (c i) t -> p c t i", i=RUN),
                in_=rounded[:, :, lo:hi].rearrange("p t (c i) -> p c t i", i=RUN),
            )
            nc.vector.quantize_mx(
                out=y_codes[:, lo:hi].bitcast(FP8X4),
                scales=y_scale[:, lo:hi],
                in_=woven[:].rearrange("p c t -> p (c t)"),
            )
            nc.sync.dma_start(out=out_words[:, lo:hi], in_=y_codes[:, lo:hi])
        for q in range(QUADRANTS):
            queue = nc.scalar if q < QUADRANTS - 1 else nc.sync
            queue.dma_start(
                out=out_2[0, 4 * q : 4 * q + 4, :].bitcast(I32), in_=y_scale[32 * q : 32 * q + 4, :].bitcast(I32)
            )
